import numpy as np
import ml_dtypes

BF16 = ml_dtypes.bfloat16


def bf(x):
    return np.asarray(x, np.float32).astype(BF16)


def f32(x):
    return np.asarray(x, np.float32)


def f64(x):
    return np.asarray(x).astype(np.float64)


def striped(idx):
    return np.tile(idx.reshape(-1, 16).T, (8, 1))


S, K, M, N, V, D = 512, 256, 256, 256, 8, 32


def setup_inputs():
    return {"table": bf(np.random.standard_normal((K, S))), "w": bf(2.0 * np.random.standard_normal((K, M)) / np.sqrt(K)), "offs": striped(np.random.permutation(np.tile(np.arange(S), 2))[:N])}


def reference(table, w, offs):
    idx = offs[:16].T.reshape(-1)
    x = f64(table)[:, idx]
    u = (f64(w).T @ x).reshape(M, V, D)
    u = u - u.max(axis=2, keepdims=True)
    p = np.exp(u)
    return (p / p.sum(axis=2, keepdims=True)).reshape(M, N)

@@ -1,0 +1,53 @@
+import concourse.mybir as mybir
+
+P = 128
+S, K, M, N, SLATES, SLATE = 512, 256, 256, 256, 8, 32
+K_BLOCKS, M_BLOCKS = K // P, M // P
+FLOPS = 2 * K * M * N
+
+BF16, F32, U16 = mybir.dt.bfloat16, mybir.dt.float32, mybir.dt.uint16
+ALU = mybir.AluOpType
+EXP = mybir.ActivationFunctionType.Exp
+X = mybir.AxisListType.X
+
+
+def tile_rows_slate_prob_rep_kernel(tc, table, w, offs, out):
+    nc = tc.nc
+    with (
+        tc.tile_pool(name="held", bufs=1) as held,
+        tc.tile_pool(name="work", bufs=M_BLOCKS) as work,
+        tc.psum_pool(name="psum", bufs=M_BLOCKS) as psum,
+    ):
+        offsets = held.tile([P, N // 16], U16, name="offsets")
+        items = held.tile([P, K_BLOCKS, S], BF16, name="items")
+        states = held.tile([P, K_BLOCKS, M], BF16, name="states")
+        nc.sync.dma_start(offsets[:], offs)
+        nc.sync.dma_start(items[:], table.rearrange("(p b) s -> p b s", b=K_BLOCKS))
+        nc.scalar.dma_start(states[:], w.rearrange("(p b) m -> p b m", b=K_BLOCKS))
+
+        def per_slate(stat):
+            return stat[:].unsqueeze(2).to_broadcast([P, SLATES, SLATE])
+
+        for a in range(M_BLOCKS):
+            scores = psum.tile([P, SLATES, SLATE], F32, name="scores")
+            for b in range(K_BLOCKS):
+                nc.tensor.matmul(
+                    scores[:].rearrange("p v t -> p (v t)"),
+                    states[:, b, a * P:(a + 1) * P],
+                    items[:, b, :].indirect(offsets[:]),
+                    start=(b == 0),
+                    stop=(b == K_BLOCKS - 1),
+                )
+            top = work.tile([P, SLATES], F32, name="top")
+            shifted = work.tile([P, SLATES, SLATE], F32, name="shifted")
+            weights = work.tile([P, SLATES, SLATE], F32, name="weights")
+            total = work.tile([P, SLATES], F32, name="total")
+            inverse = work.tile([P, SLATES], F32, name="inverse")
+            probs = work.tile([P, SLATES, SLATE], F32, name="probs")
+            nc.vector.tensor_reduce(top[:], scores[:], X, ALU.max)
+            nc.vector.tensor_tensor(shifted[:], scores[:], per_slate(top), ALU.subtract)
+            nc.scalar.activation(weights[:], shifted[:], EXP)
+            nc.vector.tensor_reduce(total[:], weights[:], X, ALU.add)
+            nc.vector.reciprocal(inverse[:], total[:])
+            nc.vector.tensor_tensor(probs[:], weights[:], per_slate(inverse), ALU.mult)
+            nc.sync.dma_start(out[a * P:(a + 1) * P, :], probs[:].rearrange("p v t -> p (v t)"))

@@ -1,8 +1,11 @@
 import concourse.mybir as mybir
 
 P = 128
-S, K, M, N, SLATES, SLATE = 512, 256, 256, 256, 8, 32
+S, K, M, N, SLATE = 512, 256, 256, 256, 32
 K_BLOCKS, M_BLOCKS = K // P, M // P
+SLATES = N // SLATE
+HALVES = 2
+HALF_COLS, HALF_SLATES = N // HALVES, SLATES // HALVES
 FLOPS = 2 * K * M * N
 
 BF16, F32, U16 = mybir.dt.bfloat16, mybir.dt.float32, mybir.dt.uint16
@@ -16,38 +19,37 @@ def tile_rows_slate_prob_rep_kernel(tc, table, w, offs, out):
     with (
         tc.tile_pool(name="held", bufs=1) as held,
         tc.tile_pool(name="work", bufs=M_BLOCKS) as work,
-        tc.psum_pool(name="psum", bufs=M_BLOCKS) as psum,
+        tc.psum_pool(name="psum", bufs=M_BLOCKS * HALVES) as psum,
     ):
         offsets = held.tile([P, N // 16], U16, name="offsets")
         items = held.tile([P, K_BLOCKS, S], BF16, name="items")
         states = held.tile([P, K_BLOCKS, M], BF16, name="states")
-        nc.sync.dma_start(offsets[:], offs)
         nc.sync.dma_start(items[:], table.rearrange("(p b) s -> p b s", b=K_BLOCKS))
+        nc.sync.dma_start(offsets[:], offs)
         nc.scalar.dma_start(states[:], w.rearrange("(p b) m -> p b m", b=K_BLOCKS))
 
-        def per_slate(stat):
-            return stat[:].unsqueeze(2).to_broadcast([P, SLATES, SLATE])
-
         for a in range(M_BLOCKS):
-            scores = psum.tile([P, SLATES, SLATE], F32, name="scores")
-            for b in range(K_BLOCKS):
-                nc.tensor.matmul(
-                    scores[:].rearrange("p v t -> p (v t)"),
-                    states[:, b, a * P:(a + 1) * P],
-                    items[:, b, :].indirect(offsets[:]),
-                    start=(b == 0),
-                    stop=(b == K_BLOCKS - 1),
-                )
-            top = work.tile([P, SLATES], F32, name="top")
-            shifted = work.tile([P, SLATES, SLATE], F32, name="shifted")
-            weights = work.tile([P, SLATES, SLATE], F32, name="weights")
+            minus_top = work.tile([P, SLATES], F32, name="minus_top")
             total = work.tile([P, SLATES], F32, name="total")
             inverse = work.tile([P, SLATES], F32, name="inverse")
+            exps = work.tile([P, SLATES, SLATE], F32, name="exps")
             probs = work.tile([P, SLATES, SLATE], F32, name="probs")
-            nc.vector.tensor_reduce(top[:], scores[:], X, ALU.max)
-            nc.vector.tensor_tensor(shifted[:], scores[:], per_slate(top), ALU.subtract)
-            nc.scalar.activation(weights[:], shifted[:], EXP)
-            nc.vector.tensor_reduce(total[:], weights[:], X, ALU.add)
+            for h in range(HALVES):
+                scores = psum.tile([P, HALF_SLATES, SLATE], F32, name="scores")
+                for b in range(K_BLOCKS):
+                    nc.tensor.matmul(
+                        scores[:].rearrange("p v t -> p (v t)"),
+                        states[:, b, a * P:(a + 1) * P],
+                        items[:, b, :].indirect(offsets[:, h * HALF_COLS // 16:(h + 1) * HALF_COLS // 16]),
+                        start=(b == 0),
+                        stop=(b == K_BLOCKS - 1),
+                    )
+                first = h * HALF_SLATES
+                nc.vector.tensor_reduce(minus_top[:, first:first + HALF_SLATES], scores[:], X, ALU.max, negate=True)
+                for v in range(first, first + HALF_SLATES):
+                    nc.scalar.activation(exps[:, v, :], scores[:, v - first, :], EXP,
+                                         bias=minus_top[:, v:v + 1], accum_out=total[:, v:v + 1])
             nc.vector.reciprocal(inverse[:], total[:])
-            nc.vector.tensor_tensor(probs[:], weights[:], per_slate(inverse), ALU.mult)
+            nc.vector.tensor_tensor(probs[:], exps[:],
+                                    inverse[:].unsqueeze(2).to_broadcast([P, SLATES, SLATE]), ALU.mult)
             nc.sync.dma_start(out[a * P:(a + 1) * P, :], probs[:].rearrange("p v t -> p (v t)"))

import concourse.mybir as mybir

P = 128
S, K, M, N, SLATE = 512, 256, 256, 256, 32
K_BLOCKS, M_BLOCKS = K // P, M // P
SLATES = N // SLATE
HALVES = 2
HALF_COLS, HALF_SLATES = N // HALVES, SLATES // HALVES
FLOPS = 2 * K * M * N

BF16, F32, U16 = mybir.dt.bfloat16, mybir.dt.float32, mybir.dt.uint16
ALU = mybir.AluOpType
EXP = mybir.ActivationFunctionType.Exp
X = mybir.AxisListType.X


def tile_rows_slate_prob_rep_kernel(tc, table, w, offs, out):
    nc = tc.nc
    with (
        tc.tile_pool(name="held", bufs=1) as held,
        tc.tile_pool(name="work", bufs=M_BLOCKS) as work,
        tc.psum_pool(name="psum", bufs=M_BLOCKS * HALVES) as psum,
    ):
        offsets = held.tile([P, N // 16], U16, name="offsets")
        items = held.tile([P, K_BLOCKS, S], BF16, name="items")
        states = held.tile([P, K_BLOCKS, M], BF16, name="states")
        nc.sync.dma_start(items[:], table.rearrange("(p b) s -> p b s", b=K_BLOCKS))
        nc.sync.dma_start(offsets[:], offs)
        nc.scalar.dma_start(states[:], w.rearrange("(p b) m -> p b m", b=K_BLOCKS))

        for a in range(M_BLOCKS):
            minus_top = work.tile([P, SLATES], F32, name="minus_top")
            total = work.tile([P, SLATES], F32, name="total")
            inverse = work.tile([P, SLATES], F32, name="inverse")
            exps = work.tile([P, SLATES, SLATE], F32, name="exps")
            probs = work.tile([P, SLATES, SLATE], F32, name="probs")
            for h in range(HALVES):
                scores = psum.tile([P, HALF_SLATES, SLATE], F32, name="scores")
                for b in range(K_BLOCKS):
                    nc.tensor.matmul(
                        scores[:].rearrange("p v t -> p (v t)"),
                        states[:, b, a * P:(a + 1) * P],
                        items[:, b, :].indirect(offsets[:, h * HALF_COLS // 16:(h + 1) * HALF_COLS // 16]),
                        start=(b == 0),
                        stop=(b == K_BLOCKS - 1),
                    )
                first = h * HALF_SLATES
                nc.vector.tensor_reduce(minus_top[:, first:first + HALF_SLATES], scores[:], X, ALU.max, negate=True)
                for v in range(first, first + HALF_SLATES):
                    nc.scalar.activation(exps[:, v, :], scores[:, v - first, :], EXP,
                                         bias=minus_top[:, v:v + 1], accum_out=total[:, v:v + 1])
            nc.vector.reciprocal(inverse[:], total[:])
            nc.vector.tensor_tensor(probs[:], exps[:],
                                    inverse[:].unsqueeze(2).to_broadcast([P, SLATES, SLATE]), ALU.mult)
            nc.sync.dma_start(out[a * P:(a + 1) * P, :], probs[:].rearrange("p v t -> p (v t)"))
